import numpy as np, ml_dtypes
CORES = [32,160,288,416,80,208,336,464]
N = 8
RM, R, T = 131072, 8192, 1024
CAPP = 256
def entries(a): return a.T.reshape(-1)
def pack(v, P): return np.ascontiguousarray(np.asarray(v, np.int32).reshape(-1, P).T)
def owners(rng, how):
    if how == "alike": return np.stack([rng.permutation(np.repeat(rng.permutation(N)[:T // CAPP], CAPP)) for r in range(N)])
    if how == "full": p = np.repeat(rng.permutation(N)[:T // CAPP], CAPP); return np.stack([rng.permutation(p) for r in range(N)])
    return np.stack([rng.permutation(np.repeat(np.arange(N), CAPP))[:T] for r in range(N)])
def lists(rng, how):
    M = rng.integers(0, N * R, N * RM)
    O1 = owners(rng, how); O2 = rng.permutation(N)[O1] if how in ("alike", "full") else owners(rng, "uniform")
    sl = np.stack([1 + rng.permutation(RM - 2)[:N * T] for o in range(N)])
    if how == "edge": sl[:, 0] = 0; sl[:, 1] = RM - 1
    I = np.zeros((N, T), np.int64); took = np.zeros(N, np.int64)
    for r in range(N):
        for o in range(N): m = np.nonzero(O1[r] == o)[0]; I[r, m] = RM * o + sl[o, took[o]:took[o] + len(m)]; took[o] += len(m)
    A = R * O2 + (np.where(rng.random((N, T)) < 0.5, 0, R - 1) if how == "edge" else rng.integers(0, R, (N, T)))
    if how == "alike": I = RM * O1 + sl[O1, 0]; A = R * O2 + rng.integers(0, R, N)[O1]
    M[I.reshape(-1)] = A.reshape(-1)
    if how == "sorted": I = np.sort(I, axis=1)
    if how == "full":
        I[1::3] = np.sort(I[1::3], axis=1); I[2::3] = np.sort(I[2::3], axis=1).reshape(-1, 16, T // 16).transpose(0, 2, 1).reshape(-1, T)
    return {"mp": np.stack([pack(m, 16) for m in M.reshape(N, RM)]), "idx": np.stack([pack(i, 16) for i in I])}
def setup_inputs(rng):
    return dict({"tab": rng.standard_normal((N, 128, R), dtype=np.float32).astype(ml_dtypes.bfloat16)}, **lists(rng, "uniform"))
def setup_inputs_alike(rng):
    d = setup_inputs(rng); d.update(lists(rng, "alike"))
    for k in ("tab",): d[k] = (d[k].astype(np.float32) * 1048576.0).astype(d[k].dtype)
    return d
def setup_inputs_edge(rng):
    d = setup_inputs(rng); d.update(lists(rng, "edge"))
    for k in ("tab",): d[k] = (d[k].astype(np.float32) * (1 / 1024.0)).astype(d[k].dtype)
    return d
def setup_inputs_full(rng):
    d = setup_inputs(rng); d.update(lists(rng, "full"))
    return d
def setup_inputs_sorted(rng):
    d = setup_inputs(rng); d.update(lists(rng, "sorted"))
    return d
def check_inputs(x):
    bad = []
    if x["mp"].min() < 0 or x["mp"].max() >= N * R: bad.append("mp out of range")
    if x["idx"].min() < 0 or x["idx"].max() >= N * RM: bad.append("idx out of range")
    M = np.concatenate([entries(m) for m in x["mp"]])
    if max(int(np.bincount(entries(a) // RM, minlength=N).max()) for a in x["idx"]) > CAPP: bad.append("more than CAPP entries of a list point into one rank's part of the map")
    if max(int(np.bincount(M[entries(a)] // R, minlength=N).max()) for a in x["idx"]) > CAPP: bad.append("more than CAPP entries of a list have map values in one rank's part of the table")
    return bad
def reference(tab, mp, idx):
    A = np.concatenate(list(tab), axis=1)
    M = np.concatenate([entries(m) for m in mp])
    return {"y": np.stack([A[:, M[entries(idx[r])]] for r in range(N)])}

@@ -1,0 +1,385 @@
+from concourse.bass import DstId, RemoteDMATransfer
+from concourse.mybir import AluOpType, ActivationFunctionType
+
+OP = AluOpType
+COPY = ActivationFunctionType.Copy
+NEV = 110
+SCRATCH = {
+    "ic": ("sbuf", [128, 256], "int32"), "pc": ("sbuf", [128, 1], "int32"),
+    "ci": ("sbuf", [128, 16], "int32"), "cf": ("sbuf", [128, 16], "float32"),
+    "w2": ("sbuf", [128, 256], "bfloat16"), "ks": ("sbuf", [128, 4], "float32"),
+    "m1": ("sbuf", [128, 128], "bfloat16"), "ones": ("sbuf", [128, 128], "bfloat16"),
+    "r7": ("sbuf", [128, 64], "int32"), "rst": ("sbuf", [128, 64], "bfloat16"),
+    "m15": ("sbuf", [128, 128], "int32"), "rep": ("sbuf", [128, 128], "float32"),
+    "lk": ("sbuf", [128, 512], "float32"), "cd": ("sbuf", [128, 128], "float32"),
+    "posr": ("sbuf", [128, 64], "bfloat16"),
+    "pidx": ("sbuf", [128, 16], "int32"), "tw": ("sbuf", [128, 64], "int32"), "lm": ("sbuf", [128, 256], "uint16"),
+    "mapw": ("sbuf", [128, 4096], "int32"), "tabw": ("sbuf", [128, 8192], "bfloat16"),
+    "mk": ("sbuf", [128, 2048], "bfloat16"), "pr": ("sbuf", [128, 2048], "float32"),
+    "vs": ("sbuf", [128, 64], "float32"), "vl": ("sbuf", [128, 512], "float32"), "vq": ("sbuf", [128, 64], "float32"),
+    "fw": ("sbuf", [128, 512], "float32"), "iw": ("sbuf", [128, 320], "int32"),
+    "ff": ("sbuf", [128, 64], "bfloat16"), "fi": ("sbuf", [128, 64], "bfloat16"),
+    "aa": ("sbuf", [128, 1024], "float32"), "bb": ("sbuf", [128, 1024], "float32"),
+    "xi": ("sbuf", [128, 128], "int32"), "xm": ("sbuf", [128, 128], "int32"), "xf": ("sbuf", [128, 128], "float32"),
+    "ou": ("sbuf", [128, 128], "uint16"),
+    "fb": ("sbuf", [128, 1024], "bfloat16"), "nb": ("sbuf", [128, 768], "bfloat16"),
+    "ld": ("sbuf", [128, 2816], "bfloat16"),
+    "fr": ("sbuf", [128, 64], "bfloat16"), "fri": ("sbuf", [128, 64], "bfloat16"), "r2": ("sbuf", [128, 64], "float32"),
+    "uw": ("sbuf", [128, 56], "float32"), "cs": ("sbuf", [128, 512], "float32"), "pou": ("sbuf", [128, 64], "uint16"),
+    "yy": ("sbuf", [128, 1024], "bfloat16"),
+    "pv": ("psum", [128, 512], "float32"), "prk": ("psum", [128, 512], "float32"),
+    "px0": ("psum", [128, 512], "float32"), "px1": ("psum", [128, 512], "float32"),
+    "po0": ("psum", [128, 512], "float32"), "po1": ("psum", [128, 512], "float32"),
+    "prk2": ("psum", [128, 512], "float32"), "ppo": ("psum", [128, 512], "float32"),
+}
+SEMAPHORES = (["e%d" % k for k in range(NEV)] + ["ls", "vp", "da", "db"] + ["ix%d" % r for r in range(8)]
+              + ["vn%d" % r for r in range(8)] + ["dn%d" % r for r in range(8)])
+
+
+def roles(cores, me, topo):
+    c = cores[me]
+    near = [x for x in range(len(cores)) if x != me and topo.same_plane(c, cores[x])]
+    part = [x for x in range(len(cores)) if topo.rack(topo.host(cores[x])) != topo.rack(topo.host(c))
+            and topo.may_write(c, cores[x]) and topo.chip(cores[x]) == topo.chip(c)][0]
+    return near, part
+
+
+def places(cores, me, topo):
+    near, part = roles(cores, me, topo)
+    far = roles(cores, part, topo)[0]
+    order = [part] + near + [me] + far
+    return [order.index(o) for o in range(len(cores))]
+
+
+def rank_program(g, core, T, topo):
+    me = T.rank_of(core)
+    if me is None:
+        return
+    cores = [int(c) for c in T.cores]
+    near, part = roles(cores, me, topo)
+    far = roles(cores, part, topo)[0]
+    pos = places(cores, me, topo)
+    V, S, PE, SY = g.vector, g.scalar, g.tensor, g.sync
+    nev = [0]
+    waited = {}
+    lsum = [0]
+
+    def ev():
+        nev[0] += 1
+        return ["e%d" % (nev[0] - 1), 0]
+
+    def inc(ins, e, n=1):
+        ins.then_inc(T.sem[e[0]], n)
+        e[1] += n
+        return e
+
+    def one(ins, n=1):
+        return inc(ins, ev(), n)
+
+    def need(q, *es):
+        nm = [k for k, v in (("g", g), ("v", V), ("s", S), ("p", PE), ("y", SY)) if v is q][0]
+        for e in es:
+            if waited.get((nm, e[0]), 0) < e[1]:
+                q.wait_ge(T.sem[e[0]], e[1])
+                waited[(nm, e[0])] = e[1]
+
+    def nbits(m):
+        return bin(m).count("1")
+
+    def send(dsts, outs, src, sem):
+        m = 0xFFFF
+        ids = []
+        for d in dsts:
+            m &= topo.mask(core, cores[d])
+            rid, pid = topo.addr(cores[d], core)
+            ids.append(DstId(rid=rid, pnc=pid))
+        g.remote_dma_fused([RemoteDMATransfer(dst_ids=ids, dma_engine_mask=m, remote_sem=T.sem[sem], srcs=[src],
+                                              dsts=outs)], local_sem=T.sem.ls)
+        lsum[0] += nbits(m)
+
+    def arr(sem, src):
+        return [sem, nbits(topo.mask(cores[src], core))]
+
+    def f(k):
+        return T.fw[:, 64 * k:64 * k + 64]
+
+    def w(k):
+        return T.iw[:, 64 * k:64 * k + 64]
+
+    s1, s2, rsum, rsb, off, nf, k8, zz = [f(k) for k in range(8)]
+    vi, hh, si, lane, key = [w(k) for k in range(5)]
+    t0, t1, t2, t3 = [T.tw[:, 16 * k:16 * k + 16] for k in range(4)]
+
+    e_idx = ev()
+    inc(SY.dma_start(T.pidx[0:64, :], T.idx[:, :]), e_idx, 16)
+    inc(S.dma_start(T.pidx[64:128, :], T.idx[:, :]), e_idx, 16)
+    e_map = ev()
+    for k in range(4):
+        inc(SY.dma_start(T.mapw[16 * k:16 * k + 16, :], T.mp[0:8, :]), e_map, 16)
+        inc(S.dma_start(T.mapw[64 + 16 * k:80 + 16 * k, :], T.mp[8:16, :]), e_map, 16)
+
+    e_pc = one(g.iota(T.pc[:, :], [[1, 1]], 0, 1))
+    e_ic = one(g.iota(T.ic[:, :], [[1, 256]], 0, 0))
+    ci, cf = T.ci, T.cf
+    need(V, e_pc)
+    x = ev()
+    inc(V.tensor_scalar(ci[:, 0:1], T.pc[:, :], 1, None, OP.bitwise_and), x)
+    inc(V.tensor_scalar(ci[:, 1:2], T.pc[:, :], 1, 7, OP.logical_shift_right, OP.bitwise_and), x)
+    inc(V.tensor_scalar(ci[:, 2:3], T.pc[:, :], 3, 8, OP.logical_shift_right, OP.bitwise_and), x)
+    inc(V.tensor_scalar(ci[:, 3:4], T.pc[:, :], 4, 3, OP.logical_shift_right, OP.bitwise_and), x)
+    need(V, x)
+    x = ev()
+    inc(V.tensor_scalar(cf[:, 0:1], ci[:, 0:1], 16, 32 * me, OP.mult, OP.add), x)
+    inc(V.tensor_tensor(cf[:, 1:2], ci[:, 1:2], ci[:, 2:3], OP.add), x)
+    inc(V.tensor_copy(cf[:, 3:4], ci[:, 3:4]), x)
+    need(V, x)
+    x = one(V.tensor_tensor(cf[:, 2:3], cf[:, 0:1], cf[:, 1:2], OP.add))
+    need(V, x, e_ic)
+    e_w2 = one(V.tensor_scalar(T.w2[:, :], T.ic[:, :], cf[:, 2:3], None, OP.is_equal))
+    e_ks = one(V.tensor_scalar(T.ks[:, :], T.ic[:, 0:4], cf[:, 3:4], None, OP.is_equal))
+
+    need(V, e_idx)
+    xb, xa = ev(), ev()
+    inc(V.tensor_scalar(t1, T.pidx[:, :], 12, 240, OP.logical_shift_right, OP.bitwise_and), xb)
+    inc(V.tensor_scalar(t2, T.pidx[:, :], 15, None, OP.bitwise_and), xb)
+    inc(V.tensor_scalar(t0, T.pidx[:, :], 4, 4095, OP.logical_shift_right, OP.bitwise_and), xa)
+    need(V, xb)
+    xc = one(V.tensor_tensor(t3, t1, t2, OP.add))
+    need(V, xa)
+    e_msg = ev()
+    lo = 32 * me
+    inc(V.tensor_copy(T.lm[:, lo:lo + 16], t0), e_msg)
+    need(V, xc)
+    inc(V.tensor_copy(T.lm[:, lo + 16:lo + 32], t3), e_msg)
+
+    need(g, e_msg)
+    own_msg = T.lm[:, lo:lo + 32]
+    send([part] + near, [own_msg] * 4, own_msg, "ix%d" % me)
+    e_ix = {o: arr("ix%d" % o, part if o in far else o) for o in range(8) if o != me}
+    need(g, e_ix[part])
+    pm = T.lm[:, 32 * part:32 * part + 32]
+    send(near, [pm] * 3, pm, "ix%d" % part)
+    for o in far:
+        e_ix[o] = arr("ix%d" % o, near[0])
+    gate0 = ev()
+    g.sem_inc(T.sem[gate0[0]], 1)
+    gate0[1] = 1
+    e_tab = ev()
+    need(SY, gate0)
+    inc(SY.dma_start(T.tabw[:, 0:4096], T.tab[:, 0:4096]), e_tab, 16)
+
+    x = ev()
+    e_pf = one(V.tensor_copy(cf[:, 4:5], T.pc[:, :]))
+    inc(V.tensor_scalar(ci[:, 5:6], T.pc[:, :], 2, 3, OP.logical_shift_right, OP.bitwise_and), x)
+    inc(V.tensor_scalar(ci[:, 6:7], T.pc[:, :], 3, None, OP.bitwise_and), x)
+    inc(V.tensor_scalar(ci[:, 7:8], T.pc[:, :], 4, None, OP.logical_shift_right), x)
+    inc(V.tensor_scalar(T.r7[:, :], T.ic[:, 0:64], 7, None, OP.bitwise_and), x)
+    inc(V.tensor_scalar(T.m15[:, :], T.ic[:, 0:128], 15, None, OP.bitwise_and), x)
+    need(V, e_pf, x)
+    e_c1, x = ev(), ev()
+    inc(V.tensor_scalar(T.m1[:, :], T.ic[:, 0:128], cf[:, 4:5], -1.0, OP.is_le, OP.mult), e_c1)
+    inc(V.memset(T.ones[:, :], 1.0), e_c1)
+    inc(V.tensor_scalar(T.rst[:, :], T.r7[:, :], 0, None, OP.is_gt), e_c1)
+    inc(V.tensor_scalar(T.rep[0:16, :], T.m15[0:16, :], cf[0:16, 4:5], None, OP.is_equal), e_c1)
+    inc(V.tensor_copy(cf[:, 5:6], ci[:, 5:6]), x)
+    inc(V.tensor_scalar(cf[:, 6:7], ci[:, 6:7], 16, None, OP.mult), x)
+    need(V, x)
+    x = one(V.tensor_tensor(cf[:, 7:8], cf[:, 6:7], ci[:, 7:8], OP.add))
+    e_c2 = ev()
+    for k in range(4):
+        inc(V.tensor_scalar(T.lk[:, 128 * k:128 * k + 128], T.m15[:, :], cf[:, 5:6], 4 * k, OP.subtract, OP.is_equal), e_c2)
+    need(V, x)
+    for d in range(2):
+        inc(V.tensor_scalar(T.cd[:, 64 * d:64 * d + 64], T.ic[:, 0:64], cf[:, 7:8], 8 * d, OP.subtract, OP.is_equal), e_c2)
+    for o in range(8):
+        inc(V.memset(T.posr[:, 8 * o:8 * o + 8], 2.0 * pos[o]), e_c2)
+
+    need(S, e_w2)
+    need(PE, e_ks)
+    need(V, e_map)
+    e_pv = ev()
+    for i in [me] + near + [part] + far:
+        src = e_msg if i == me else e_ix[i]
+        b, mb = 32 * i, 256 * i
+        need(S, src)
+        xm = one(S.activation(T.mk[:, mb:mb + 256], T.w2[:, :].indirect(T.lm[:, b + 16:b + 32]), COPY))
+        need(V, src, xm)
+        xp = one(V.tensor_tensor(T.pr[:, mb:mb + 256], T.mapw[:, :].indirect(T.lm[:, b:b + 16]), T.mk[:, mb:mb + 256], OP.mult))
+        need(PE, xp)
+        for d in range(2):
+            c0 = 8 * i + 4 * d
+            inc(PE.matmul(T.pv[:, c0:c0 + 4], T.pr[:, mb + 128 * d:mb + 128 * d + 128], T.ks[:, :], True, True), e_pv)
+
+    need(V, e_pv)
+    e_vs = one(V.tensor_copy(T.vs[:, :], T.pv[:, 0:64]))
+    need(g, e_vs)
+    vl = T.vl[:, 64 * me:64 * me + 64]
+    send(near, [vl] * 3, T.vs[:, :], "vn%d" % me)
+    gate1 = ev()
+    g.sem_inc(T.sem[gate1[0]], 1)
+    gate1[1] = 1
+    need(SY, gate1)
+    inc(SY.dma_start(T.tabw[:, 4096:8192], T.tab[:, 4096:8192]), e_tab, 16)
+    na, nb, nc = near
+    need(V, e_vs)
+    for o in near:
+        need(V, arr("vn%d" % o, o))
+    x = ev()
+    inc(V.tensor_tensor(s1, T.vl[:, 64 * na:64 * na + 64], T.vl[:, 64 * nb:64 * nb + 64], OP.add), x)
+    inc(V.tensor_tensor(s2, T.vs[:, :], T.vl[:, 64 * nc:64 * nc + 64], OP.add), x)
+    need(V, x)
+    e_rs = one(V.tensor_tensor(rsum, s1, s2, OP.add))
+    need(g, e_rs)
+    send([part], [T.vq[:, :]], rsum, "vp")
+    need(V, e_rs)
+    e_rb = one(V.tensor_scalar(rsb, rsum, 8192 * me, None, OP.subtract))
+    need(V, arr("vp", part))
+    x = one(V.tensor_tensor(vi, rsum, T.vq[:, :], OP.add))
+    need(V, e_rb)
+    e_off = one(V.tensor_tensor(off, rsb, T.vq[:, :], OP.add))
+
+    need(V, x)
+    e_h = one(V.tensor_scalar(hh, vi, 13, None, OP.logical_shift_right))
+    need(V, e_h, e_c1)
+    e_f = one(V.tensor_scalar(T.ff[:, :], hh, me, None, OP.is_equal))
+    e_nf = one(V.tensor_scalar(nf, hh, me, 4096, OP.not_equal, OP.mult))
+    need(V, e_f)
+    e_fi = one(V.tensor_tensor_scan(T.fi[:, :], T.rst[:, :], T.ff[:, :], 0.0, OP.mult, OP.add))
+    need(PE, e_c1, e_f)
+    PE.matmul(T.prk[:, 0:64], T.m1[:, :], T.ff[:, :], True, False)
+    need(PE, e_fi)
+    e_rk = one(PE.matmul(T.prk[:, 0:64], T.ones[:, :], T.fi[:, :], False, True))
+    need(V, e_rk, e_nf)
+    x = one(V.tensor_tensor(si, T.prk[:, 0:64], nf, OP.add))
+    need(V, x)
+    xl = one(V.tensor_scalar(lane, si, 4096 + 15, None, OP.bitwise_and))
+    xk = one(V.tensor_scalar(key, si, 4, None, OP.logical_shift_right))
+    e_ab = ev()
+
+    def lanes(m0, m1):
+        for m in range(m0, m1):
+            inc(V.tensor_scalar(T.aa[:, 64 * m:64 * m + 64], lane, m, None, OP.is_equal), e_ab)
+
+    need(V, xl)
+    lanes(0, 4)
+    need(V, xk)
+    x8 = one(V.tensor_scalar(k8, key, 8192, None, OP.mult))
+    lanes(4, 8)
+    need(V, x8, e_off)
+    xz = one(V.tensor_tensor(zz, k8, off, OP.add))
+    lanes(8, 16)
+    need(V, xz)
+    for n in range(16):
+        inc(V.tensor_scalar(T.bb[:, 64 * n:64 * n + 64], zz, 8192 * n, 8192 * n + 8192, OP.max, OP.min), e_ab)
+    need(PE, e_ab)
+    batches = [far + [part], near + [me]]
+    px, po = [T.px0, T.px1], [T.po0, T.po1]
+    e_x, e_o, e_xf, e_ou = [ev(), ev()], [None, None], [None, None], [None, None]
+
+    def pack(b):
+        for j, i in enumerate(batches[b]):
+            for c in range(8):
+                col = 8 * i + c
+                ins = PE.matmul(px[b][0:16, 16 * j:16 * j + 16], T.aa[:, col:1024:64], T.bb[:, col:1024:64], c == 0, c == 7)
+            inc(ins, e_x[b])
+
+    def strip(b):
+        s = slice(64 * b, 64 * b + 64)
+        need(V, e_x[b])
+        x = one(V.tensor_copy(T.xi[0:16, s], px[b][0:16, 0:64]))
+        need(V, x)
+        x = one(V.tensor_scalar(T.xm[0:16, s], T.xi[0:16, s], 8191, None, OP.bitwise_and))
+        need(V, x)
+        e_xf[b] = one(V.tensor_copy(T.xf[0:16, s], T.xm[0:16, s]))
+
+    def spread(b):
+        need(PE, e_xf[b])
+        e_o[b] = one(PE.matmul(po[b][:, 0:64], T.rep[0:16, :], T.xf[0:16, 64 * b:64 * b + 64], True, True))
+
+    def offsets(b):
+        need(V, e_o[b])
+        e_ou[b] = one(V.tensor_copy(T.ou[:, 64 * b:64 * b + 64], po[b][:, 0:64]))
+
+    def cols(b, j):
+        return T.tabw[:, :].indirect(T.ou[:, 64 * b + 16 * j:64 * b + 16 * j + 16])
+
+    pack(0)
+    strip(0)
+    spread(0)
+    offsets(0)
+    pack(1)
+    need(V, e_ou[0], e_tab)
+    need(S, e_ou[0], e_tab)
+    e_w = [ev(), ev()]
+    for q in range(2):
+        inc(V.tensor_copy(T.fb[:, 512 * q:512 * q + 256], cols(0, 2 * q)), e_w[q])
+        inc(S.activation(T.fb[:, 512 * q + 256:512 * q + 512], cols(0, 2 * q + 1), COPY), e_w[q])
+    strip(1)
+    spread(1)
+    offsets(1)
+    need(V, e_ou[1])
+    need(S, e_ou[1])
+    ow = 768 + 256 * pos[me]
+    e_n = []
+    e_n.append(one(V.tensor_copy(T.nb[:, 0:256], cols(1, 0))))
+    e_n.append(one(S.activation(T.nb[:, 256:512], cols(1, 1), COPY)))
+    e_n.append(one(V.tensor_copy(T.nb[:, 512:768], cols(1, 2))))
+    e_own = one(S.activation(T.ld[:, ow:ow + 256], cols(1, 3), COPY))
+    for q, sem in enumerate(("da", "db")):
+        need(g, e_w[q])
+        blk = slice(512 * q, 512 * q + 512)
+        send([part], [T.ld[:, blk]], T.fb[:, blk], sem)
+    for j, o in enumerate(near):
+        need(g, e_n[j])
+        at = 768 + 256 * places(cores, o, topo)[me]
+        send([o], [T.ld[:, at:at + 256]], T.nb[:, 256 * j:256 * j + 256], "dn%d" % me)
+    e_d = [arr("da", part), arr("db", part)]
+    for j, o in enumerate(near):
+        need(g, e_d[j // 2])
+        at = 768 + 256 * places(cores, o, topo)[part]
+        send([o], [T.ld[:, at:at + 256]], T.ld[:, 256 * j:256 * j + 256], "dn%d" % part)
+
+    e_fr = ev()
+    hm = T.iw[:, 64 + 8 * me:72 + 8 * me]
+    for o in range(8):
+        inc(V.tensor_scalar(T.fr[:, 8 * o:8 * o + 8], hm, o, None, OP.is_equal), e_fr)
+    need(V, e_fr)
+    e_fri = one(V.tensor_tensor_scan(T.fri[:, :], T.rst[:, :], T.fr[:, :], 0.0, OP.mult, OP.add))
+    need(PE, e_fr, e_c2)
+    PE.matmul(T.prk2[:, 0:64], T.m1[:, :], T.fr[:, :], True, False)
+    PE.matmul(T.prk2[:, 0:64], T.ones[:, :], T.posr[:, :], False, False)
+    need(PE, e_fri)
+    x = one(PE.matmul(T.prk2[:, 0:64], T.ones[:, :], T.fri[:, :], False, True))
+    need(V, x)
+    x = one(V.tensor_tensor(T.r2[:, :], T.prk2[:, 0:64], T.fr[:, :], OP.mult))
+    need(V, x)
+    x = one(V.tensor_tensor(T.uw[:, 0:32], T.r2[:, 0:32], T.r2[:, 32:64], OP.add))
+    need(V, x)
+    x = one(V.tensor_tensor(T.uw[:, 32:48], T.uw[:, 0:16], T.uw[:, 16:32], OP.add))
+    need(V, x)
+    x = one(V.tensor_tensor(T.uw[:, 48:56], T.uw[:, 32:40], T.uw[:, 40:48], OP.add))
+    need(S, x, e_c2)
+    for d in range(2):
+        for k in range(4):
+            j = 4 * d + k
+            xs = one(S.activation(T.cs[:, 64 * j:64 * j + 64], T.cd[:, 64 * d:64 * d + 64], COPY, scale=T.uw[:, 48 + j:49 + j]))
+            need(PE, xs)
+            ins = PE.matmul(T.ppo[:, 0:64], T.lk[:, 128 * k:128 * k + 128], T.cs[:, 64 * j:64 * j + 64], j == 0, j == 7)
+    e_po = one(ins)
+    need(V, e_po)
+    e_pou = one(V.tensor_copy(T.pou[:, :], T.ppo[:, 0:64]))
+    win = T.ld[:, 768:2816]
+    for q in (V, S):
+        need(q, e_pou, e_own)
+        for o in near + far:
+            need(q, arr("dn%d" % o, near[0] if o in far else o))
+        need(q, e_d[1])
+    ya = one(V.tensor_copy(T.yy[:, 0:512], win.indirect(T.pou[:, 0:32])))
+    yb = one(S.activation(T.yy[:, 512:1024], win.indirect(T.pou[:, 32:64]), COPY))
+    need(SY, ya)
+    need(S, yb)
+    e_y = ev()
+    inc(SY.dma_start(T.y[:, 0:512], T.yy[:, 0:512]), e_y, 16)
+    inc(S.dma_start(T.y[:, 512:1024], T.yy[:, 512:1024]), e_y, 16)
+    g.wait_ge(T.sem.ls, lsum[0])
+    need(g, e_y)

@@ -3,6 +3,7 @@ from concourse.mybir import AluOpType, ActivationFunctionType
 
 OP = AluOpType
 COPY = ActivationFunctionType.Copy
+RELU = ActivationFunctionType.Relu
 NEV = 110
 SCRATCH = {
     "ic": ("sbuf", [128, 256], "int32"), "pc": ("sbuf", [128, 1], "int32"),
@@ -19,11 +20,10 @@ SCRATCH = {
     "vs": ("sbuf", [128, 64], "float32"), "vl": ("sbuf", [128, 512], "float32"), "vq": ("sbuf", [128, 64], "float32"),
     "fw": ("sbuf", [128, 512], "float32"), "iw": ("sbuf", [128, 320], "int32"),
     "ff": ("sbuf", [128, 64], "bfloat16"), "fi": ("sbuf", [128, 64], "bfloat16"),
-    "aa": ("sbuf", [128, 1024], "float32"), "bb": ("sbuf", [128, 1024], "float32"),
+    "aa": ("sbuf", [128, 1024], "float32"), "bb": ("sbuf", [128, 1024], "float32"), "bt": ("sbuf", [128, 512], "float32"),
     "xi": ("sbuf", [128, 128], "int32"), "xm": ("sbuf", [128, 128], "int32"), "xf": ("sbuf", [128, 128], "float32"),
     "ou": ("sbuf", [128, 128], "uint16"),
-    "fb": ("sbuf", [128, 1024], "bfloat16"), "nb": ("sbuf", [128, 768], "bfloat16"),
-    "ld": ("sbuf", [128, 2816], "bfloat16"),
+    "fb": ("sbuf", [128, 2048], "bfloat16"), "ld": ("sbuf", [128, 2048], "bfloat16"),
     "fr": ("sbuf", [128, 64], "bfloat16"), "fri": ("sbuf", [128, 64], "bfloat16"), "r2": ("sbuf", [128, 64], "float32"),
     "uw": ("sbuf", [128, 56], "float32"), "cs": ("sbuf", [128, 512], "float32"), "pou": ("sbuf", [128, 64], "uint16"),
     "yy": ("sbuf", [128, 1024], "bfloat16"),
@@ -32,37 +32,70 @@ SCRATCH = {
     "po0": ("psum", [128, 512], "float32"), "po1": ("psum", [128, 512], "float32"),
     "prk2": ("psum", [128, 512], "float32"), "ppo": ("psum", [128, 512], "float32"),
 }
-SEMAPHORES = (["e%d" % k for k in range(NEV)] + ["ls", "vp", "da", "db"] + ["ix%d" % r for r in range(8)]
+SEMAPHORES = (["e%d" % k for k in range(NEV)] + ["ls", "vp", "hx"] + ["ix%d" % r for r in range(8)]
               + ["vn%d" % r for r in range(8)] + ["dn%d" % r for r in range(8)])
 
 
 def roles(cores, me, topo):
     c = cores[me]
     near = [x for x in range(len(cores)) if x != me and topo.same_plane(c, cores[x])]
-    part = [x for x in range(len(cores)) if topo.rack(topo.host(cores[x])) != topo.rack(topo.host(c))
-            and topo.may_write(c, cores[x]) and topo.chip(cores[x]) == topo.chip(c)][0]
-    return near, part
+    far = [x for x in range(len(cores)) if x != me and x not in near]
+    part = [x for x in far if topo.may_write(c, cores[x]) and topo.chip(cores[x]) == topo.chip(c)][0]
+    cross = [x for x in far if topo.may_write(c, cores[x]) and x != part][0]
+    diag = [x for x in far if not topo.may_write(c, cores[x])]
+    return near, part, cross, diag
+
+
+def helpers(c, topo):
+    return [h for h in range(512) if topo.host(h) == topo.host(c) and topo.chip(h) == topo.chip(c)
+            and topo.die(h) != topo.die(c)][:2]
 
 
 def places(cores, me, topo):
-    near, part = roles(cores, me, topo)
-    far = roles(cores, part, topo)[0]
-    order = [part] + near + [me] + far
+    near, part, cross, diag = roles(cores, me, topo)
+    order = [part, cross] + near + [me] + diag
     return [order.index(o) for o in range(len(cores))]
 
 
+def nbits(m):
+    return bin(m).count("1")
+
+
 def rank_program(g, core, T, topo):
+    cores = [int(c) for c in T.cores]
+    lsum = [0]
+
+    def send(dsts, outs, src, sem):
+        m = 0xFFFF
+        ids = []
+        for d in dsts:
+            m &= topo.mask(core, d)
+            rid, pid = topo.addr(d, core)
+            ids.append(DstId(rid=rid, pnc=pid))
+        g.remote_dma_fused([RemoteDMATransfer(dst_ids=ids, dma_engine_mask=m, remote_sem=T.sem[sem], srcs=[src],
+                                              dsts=outs)], local_sem=T.sem.ls)
+        lsum[0] += nbits(m)
+
+    def block(o, t):
+        at = 256 * places(cores, o, topo)[t]
+        return T.ld[:, at:at + 256]
+
     me = T.rank_of(core)
     if me is None:
+        own = [r for r in range(8) if topo.host(cores[r]) == topo.host(core) and topo.chip(cores[r]) == topo.chip(core)]
+        if own and core in helpers(cores[own[0]], topo):
+            p = roles(cores, own[0], topo)[1]
+            to = roles(cores, p, topo)[3][helpers(cores[own[0]], topo).index(core)]
+            g.wait_ge(T.sem.hx, nbits(topo.mask(cores[p], core)))
+            send([cores[to]], [block(to, p)], T.fb[:, 0:256], "dn%d" % p)
+            g.wait_ge(T.sem.ls, lsum[0])
         return
-    cores = [int(c) for c in T.cores]
-    near, part = roles(cores, me, topo)
-    far = roles(cores, part, topo)[0]
+    near, part, cross, diag = roles(cores, me, topo)
+    passed = roles(cores, part, topo)[3]
     pos = places(cores, me, topo)
     V, S, PE, SY = g.vector, g.scalar, g.tensor, g.sync
     nev = [0]
     waited = {}
-    lsum = [0]
 
     def ev():
         nev[0] += 1
@@ -83,21 +116,8 @@ def rank_program(g, core, T, topo):
                 q.wait_ge(T.sem[e[0]], e[1])
                 waited[(nm, e[0])] = e[1]
 
-    def nbits(m):
-        return bin(m).count("1")
-
-    def send(dsts, outs, src, sem):
-        m = 0xFFFF
-        ids = []
-        for d in dsts:
-            m &= topo.mask(core, cores[d])
-            rid, pid = topo.addr(cores[d], core)
-            ids.append(DstId(rid=rid, pnc=pid))
-        g.remote_dma_fused([RemoteDMATransfer(dst_ids=ids, dma_engine_mask=m, remote_sem=T.sem[sem], srcs=[src],
-                                              dsts=outs)], local_sem=T.sem.ls)
-        lsum[0] += nbits(m)
-
-    def arr(sem, src):
+    def arr(sem, o):
+        src = o if topo.may_write(cores[o], core) else roles(cores, o, topo)[1]
         return [sem, nbits(topo.mask(cores[src], core))]
 
     def f(k):
@@ -154,13 +174,11 @@ def rank_program(g, core, T, topo):
 
     need(g, e_msg)
     own_msg = T.lm[:, lo:lo + 32]
-    send([part] + near, [own_msg] * 4, own_msg, "ix%d" % me)
-    e_ix = {o: arr("ix%d" % o, part if o in far else o) for o in range(8) if o != me}
+    send([cores[o] for o in [part, cross] + near], [own_msg] * 5, own_msg, "ix%d" % me)
+    e_ix = {o: arr("ix%d" % o, o) for o in range(8) if o != me}
     need(g, e_ix[part])
     pm = T.lm[:, 32 * part:32 * part + 32]
-    send(near, [pm] * 3, pm, "ix%d" % part)
-    for o in far:
-        e_ix[o] = arr("ix%d" % o, near[0])
+    send([cores[o] for o in passed], [pm] * 2, pm, "ix%d" % part)
     gate0 = ev()
     g.sem_inc(T.sem[gate0[0]], 1)
     gate0[1] = 1
@@ -198,7 +216,7 @@ def rank_program(g, core, T, topo):
     need(PE, e_ks)
     need(V, e_map)
     e_pv = ev()
-    for i in [me] + near + [part] + far:
+    for i in [me] + near + [part, cross] + diag:
         src = e_msg if i == me else e_ix[i]
         b, mb = 32 * i, 256 * i
         need(S, src)
@@ -214,7 +232,7 @@ def rank_program(g, core, T, topo):
     e_vs = one(V.tensor_copy(T.vs[:, :], T.pv[:, 0:64]))
     need(g, e_vs)
     vl = T.vl[:, 64 * me:64 * me + 64]
-    send(near, [vl] * 3, T.vs[:, :], "vn%d" % me)
+    send([cores[o] for o in near], [vl] * 3, T.vs[:, :], "vn%d" % me)
     gate1 = ev()
     g.sem_inc(T.sem[gate1[0]], 1)
     gate1[1] = 1
@@ -230,13 +248,13 @@ def rank_program(g, core, T, topo):
     need(V, x)
     e_rs = one(V.tensor_tensor(rsum, s1, s2, OP.add))
     need(g, e_rs)
-    send([part], [T.vq[:, :]], rsum, "vp")
+    send([cores[part]], [T.vq[:, :]], rsum, "vp")
     need(V, e_rs)
-    e_rb = one(V.tensor_scalar(rsb, rsum, 8192 * me, None, OP.subtract))
+    e_rb = one(V.tensor_scalar(rsb, rsum, -1, 8192 * me, OP.mult, OP.add))
     need(V, arr("vp", part))
     x = one(V.tensor_tensor(vi, rsum, T.vq[:, :], OP.add))
     need(V, e_rb)
-    e_off = one(V.tensor_tensor(off, rsb, T.vq[:, :], OP.add))
+    e_off = one(V.tensor_tensor(off, rsb, T.vq[:, :], OP.subtract))
 
     need(V, x)
     e_h = one(V.tensor_scalar(hh, vi, 13, None, OP.logical_shift_right))
@@ -252,41 +270,46 @@ def rank_program(g, core, T, topo):
     need(V, e_rk, e_nf)
     x = one(V.tensor_tensor(si, T.prk[:, 0:64], nf, OP.add))
     need(V, x)
-    xl = one(V.tensor_scalar(lane, si, 4096 + 15, None, OP.bitwise_and))
     xk = one(V.tensor_scalar(key, si, 4, None, OP.logical_shift_right))
-    e_ab = ev()
+    xl = one(V.tensor_scalar(lane, si, 4096 + 15, None, OP.bitwise_and))
+    e_ab = [ev(), ev()]
 
     def lanes(m0, m1):
         for m in range(m0, m1):
-            inc(V.tensor_scalar(T.aa[:, 64 * m:64 * m + 64], lane, m, None, OP.is_equal), e_ab)
+            inc(V.tensor_scalar(T.aa[:, 64 * m:64 * m + 64], lane, m, None, OP.is_equal), e_ab[0])
 
-    need(V, xl)
-    lanes(0, 4)
     need(V, xk)
-    x8 = one(V.tensor_scalar(k8, key, 8192, None, OP.mult))
-    lanes(4, 8)
+    x8 = one(V.tensor_scalar(k8, key, -8192, None, OP.mult))
+    need(V, xl)
+    lanes(0, 1)
     need(V, x8, e_off)
     xz = one(V.tensor_tensor(zz, k8, off, OP.add))
-    lanes(8, 16)
+    lanes(1, 16)
     need(V, xz)
-    for n in range(16):
-        inc(V.tensor_scalar(T.bb[:, 64 * n:64 * n + 64], zz, 8192 * n, 8192 * n + 8192, OP.max, OP.min), e_ab)
-    need(PE, e_ab)
-    batches = [far + [part], near + [me]]
-    px, po = [T.px0, T.px1], [T.po0, T.po1]
-    e_x, e_o, e_xf, e_ou = [ev(), ev()], [None, None], [None, None], [None, None]
+    for n in range(8):
+        inc(V.tensor_scalar(T.bb[:, 64 * n:64 * n + 64], zz, -8192 * n - 8192, -8192 * n, OP.max, OP.min), e_ab[0])
+    need(S, xz)
+    xs = ev()
+    for n in range(8, 16):
+        inc(S.activation(T.bt[:, 64 * n - 512:64 * n - 448], zz, RELU, bias=-8192.0 * n, scale=-1.0), xs)
+    need(S, xs)
+    for n in range(8, 16):
+        inc(S.activation(T.bb[:, 64 * n:64 * n + 64], T.bt[:, 64 * n - 512:64 * n - 448], RELU, bias=8192.0, scale=-1.0), e_ab[1])
+    batches = [diag, [cross, part], near[0:2], [near[2], me]]
+    px, po = [T.px0, T.px1, T.pv, T.px0], [T.po0, T.po1, T.po0, T.po1]
+    e_x, e_o, e_xf, e_ou = [ev() for b in range(4)], [None] * 4, [None] * 4, [None] * 4
 
-    def pack(b):
-        for j, i in enumerate(batches[b]):
-            for c in range(8):
-                col = 8 * i + c
-                ins = PE.matmul(px[b][0:16, 16 * j:16 * j + 16], T.aa[:, col:1024:64], T.bb[:, col:1024:64], c == 0, c == 7)
-            inc(ins, e_x[b])
+    def pack(b, j, n0=0, n1=16):
+        for c in range(8):
+            col = 8 * batches[b][j] + c
+            ins = PE.matmul(px[b][0:16, 16 * j + n0:16 * j + n1], T.aa[:, col:1024:64],
+                            T.bb[:, 64 * n0 + col:64 * n1:64], c == 0, c == 7)
+        inc(ins, e_x[b])
 
     def strip(b):
-        s = slice(64 * b, 64 * b + 64)
+        s = slice(32 * b, 32 * b + 32)
         need(V, e_x[b])
-        x = one(V.tensor_copy(T.xi[0:16, s], px[b][0:16, 0:64]))
+        x = one(V.tensor_scalar(T.xi[0:16, s], px[b][0:16, 0:32], -1, None, OP.mult))
         need(V, x)
         x = one(V.tensor_scalar(T.xm[0:16, s], T.xi[0:16, s], 8191, None, OP.bitwise_and))
         need(V, x)
@@ -294,63 +317,66 @@ def rank_program(g, core, T, topo):
 
     def spread(b):
         need(PE, e_xf[b])
-        e_o[b] = one(PE.matmul(po[b][:, 0:64], T.rep[0:16, :], T.xf[0:16, 64 * b:64 * b + 64], True, True))
+        if b >= 2:
+            need(PE, e_ou[b - 2])
+        e_o[b] = one(PE.matmul(po[b][:, 0:32], T.rep[0:16, :], T.xf[0:16, 32 * b:32 * b + 32], True, True))
 
-    def offsets(b):
+    e_c = {}
+
+    def columns(b):
         need(V, e_o[b])
-        e_ou[b] = one(V.tensor_copy(T.ou[:, 64 * b:64 * b + 64], po[b][:, 0:64]))
+        e_ou[b] = one(V.tensor_copy(T.ou[:, 32 * b:32 * b + 32], po[b][:, 0:32]))
+        need(V, e_ou[b], e_tab)
+        need(S, e_ou[b], e_tab)
+        for j, i in enumerate(batches[b]):
+            src = T.tabw[:, :].indirect(T.ou[:, 32 * b + 16 * j:32 * b + 16 * j + 16])
+            dst = block(me, me) if i == me else T.fb[:, 512 * b + 256 * j:512 * b + 256 * j + 256]
+            e_c[i] = one(S.activation(dst, src, COPY) if j else V.tensor_copy(dst, src))
 
-    def cols(b, j):
-        return T.tabw[:, :].indirect(T.ou[:, 64 * b + 16 * j:64 * b + 16 * j + 16])
-
-    pack(0)
-    strip(0)
-    spread(0)
-    offsets(0)
-    pack(1)
-    need(V, e_ou[0], e_tab)
-    need(S, e_ou[0], e_tab)
-    e_w = [ev(), ev()]
-    for q in range(2):
-        inc(V.tensor_copy(T.fb[:, 512 * q:512 * q + 256], cols(0, 2 * q)), e_w[q])
-        inc(S.activation(T.fb[:, 512 * q + 256:512 * q + 512], cols(0, 2 * q + 1), COPY), e_w[q])
-    strip(1)
-    spread(1)
-    offsets(1)
-    need(V, e_ou[1])
-    need(S, e_ou[1])
-    ow = 768 + 256 * pos[me]
-    e_n = []
-    e_n.append(one(V.tensor_copy(T.nb[:, 0:256], cols(1, 0))))
-    e_n.append(one(S.activation(T.nb[:, 256:512], cols(1, 1), COPY)))
-    e_n.append(one(V.tensor_copy(T.nb[:, 512:768], cols(1, 2))))
-    e_own = one(S.activation(T.ld[:, ow:ow + 256], cols(1, 3), COPY))
-    for q, sem in enumerate(("da", "db")):
-        need(g, e_w[q])
-        blk = slice(512 * q, 512 * q + 512)
-        send([part], [T.ld[:, blk]], T.fb[:, blk], sem)
-    for j, o in enumerate(near):
-        need(g, e_n[j])
-        at = 768 + 256 * places(cores, o, topo)[me]
-        send([o], [T.ld[:, at:at + 256]], T.nb[:, 256 * j:256 * j + 256], "dn%d" % me)
-    e_d = [arr("da", part), arr("db", part)]
-    for j, o in enumerate(near):
-        need(g, e_d[j // 2])
-        at = 768 + 256 * places(cores, o, topo)[part]
-        send([o], [T.ld[:, at:at + 256]], T.ld[:, 256 * j:256 * j + 256], "dn%d" % part)
-
+    need(PE, e_ab[0])
+    pack(0, 0, 0, 8)
+    pack(0, 1, 0, 8)
+    need(PE, e_ab[1])
+    pack(0, 0, 8, 16)
+    pack(0, 1, 8, 16)
     e_fr = ev()
     hm = T.iw[:, 64 + 8 * me:72 + 8 * me]
     for o in range(8):
         inc(V.tensor_scalar(T.fr[:, 8 * o:8 * o + 8], hm, o, None, OP.is_equal), e_fr)
+    strip(0)
+    pack(1, 0)
+    spread(0)
+    columns(0)
+    pack(1, 1)
+    strip(1)
     need(V, e_fr)
     e_fri = one(V.tensor_tensor_scan(T.fri[:, :], T.rst[:, :], T.fr[:, :], 0.0, OP.mult, OP.add))
-    need(PE, e_fr, e_c2)
+    pack(2, 0)
+    spread(1)
+    columns(1)
+    pack(2, 1)
+    need(PE, e_fr, e_c2, e_fri)
     PE.matmul(T.prk2[:, 0:64], T.m1[:, :], T.fr[:, :], True, False)
     PE.matmul(T.prk2[:, 0:64], T.ones[:, :], T.posr[:, :], False, False)
-    need(PE, e_fri)
-    x = one(PE.matmul(T.prk2[:, 0:64], T.ones[:, :], T.fri[:, :], False, True))
-    need(V, x)
+    e_p2 = one(PE.matmul(T.prk2[:, 0:64], T.ones[:, :], T.fri[:, :], False, True))
+    strip(2)
+    pack(3, 0)
+    spread(2)
+    columns(2)
+    pack(3, 1)
+    strip(3)
+    spread(3)
+    columns(3)
+
+    for k, i in enumerate(diag + [cross, part] + near):
+        need(g, e_c[i])
+        src = T.fb[:, 256 * k:256 * k + 256]
+        if i in diag:
+            send([helpers(cores[part], topo)[k]], [T.fb[:, 0:256]], src, "hx")
+        else:
+            send([cores[i]], [block(i, me)], src, "dn%d" % me)
+
+    need(V, e_p2, e_fr)
     x = one(V.tensor_tensor(T.r2[:, :], T.prk2[:, 0:64], T.fr[:, :], OP.mult))
     need(V, x)
     x = one(V.tensor_tensor(T.uw[:, 0:32], T.r2[:, 0:32], T.r2[:, 32:64], OP.add))
@@ -368,12 +394,11 @@ def rank_program(g, core, T, topo):
     e_po = one(ins)
     need(V, e_po)
     e_pou = one(V.tensor_copy(T.pou[:, :], T.ppo[:, 0:64]))
-    win = T.ld[:, 768:2816]
+    win = T.ld[:, 0:2048]
     for q in (V, S):
-        need(q, e_pou, e_own)
-        for o in near + far:
-            need(q, arr("dn%d" % o, near[0] if o in far else o))
-        need(q, e_d[1])
+        need(q, e_pou, e_c[me])
+        for o in near + [cross, part] + diag:
+            need(q, arr("dn%d" % o, o))
     ya = one(V.tensor_copy(T.yy[:, 0:512], win.indirect(T.pou[:, 0:32])))
     yb = one(S.activation(T.yy[:, 512:1024], win.indirect(T.pou[:, 32:64]), COPY))
     need(SY, ya)

from concourse.bass import DstId, RemoteDMATransfer
from concourse.mybir import AluOpType, ActivationFunctionType

OP = AluOpType
COPY = ActivationFunctionType.Copy
RELU = ActivationFunctionType.Relu
NEV = 110
SCRATCH = {
    "ic": ("sbuf", [128, 256], "int32"), "pc": ("sbuf", [128, 1], "int32"),
    "ci": ("sbuf", [128, 16], "int32"), "cf": ("sbuf", [128, 16], "float32"),
    "w2": ("sbuf", [128, 256], "bfloat16"), "ks": ("sbuf", [128, 4], "float32"),
    "m1": ("sbuf", [128, 128], "bfloat16"), "ones": ("sbuf", [128, 128], "bfloat16"),
    "r7": ("sbuf", [128, 64], "int32"), "rst": ("sbuf", [128, 64], "bfloat16"),
    "m15": ("sbuf", [128, 128], "int32"), "rep": ("sbuf", [128, 128], "float32"),
    "lk": ("sbuf", [128, 512], "float32"), "cd": ("sbuf", [128, 128], "float32"),
    "posr": ("sbuf", [128, 64], "bfloat16"),
    "pidx": ("sbuf", [128, 16], "int32"), "tw": ("sbuf", [128, 64], "int32"), "lm": ("sbuf", [128, 256], "uint16"),
    "mapw": ("sbuf", [128, 4096], "int32"), "tabw": ("sbuf", [128, 8192], "bfloat16"),
    "mk": ("sbuf", [128, 2048], "bfloat16"), "pr": ("sbuf", [128, 2048], "float32"),
    "vs": ("sbuf", [128, 64], "float32"), "vl": ("sbuf", [128, 512], "float32"), "vq": ("sbuf", [128, 64], "float32"),
    "fw": ("sbuf", [128, 512], "float32"), "iw": ("sbuf", [128, 320], "int32"),
    "ff": ("sbuf", [128, 64], "bfloat16"), "fi": ("sbuf", [128, 64], "bfloat16"),
    "aa": ("sbuf", [128, 1024], "float32"), "bb": ("sbuf", [128, 1024], "float32"), "bt": ("sbuf", [128, 512], "float32"),
    "xi": ("sbuf", [128, 128], "int32"), "xm": ("sbuf", [128, 128], "int32"), "xf": ("sbuf", [128, 128], "float32"),
    "ou": ("sbuf", [128, 128], "uint16"),
    "fb": ("sbuf", [128, 2048], "bfloat16"), "ld": ("sbuf", [128, 2048], "bfloat16"),
    "fr": ("sbuf", [128, 64], "bfloat16"), "fri": ("sbuf", [128, 64], "bfloat16"), "r2": ("sbuf", [128, 64], "float32"),
    "uw": ("sbuf", [128, 56], "float32"), "cs": ("sbuf", [128, 512], "float32"), "pou": ("sbuf", [128, 64], "uint16"),
    "yy": ("sbuf", [128, 1024], "bfloat16"),
    "pv": ("psum", [128, 512], "float32"), "prk": ("psum", [128, 512], "float32"),
    "px0": ("psum", [128, 512], "float32"), "px1": ("psum", [128, 512], "float32"),
    "po0": ("psum", [128, 512], "float32"), "po1": ("psum", [128, 512], "float32"),
    "prk2": ("psum", [128, 512], "float32"), "ppo": ("psum", [128, 512], "float32"),
}
SEMAPHORES = (["e%d" % k for k in range(NEV)] + ["ls", "vp", "hx"] + ["ix%d" % r for r in range(8)]
              + ["vn%d" % r for r in range(8)] + ["dn%d" % r for r in range(8)])


def roles(cores, me, topo):
    c = cores[me]
    near = [x for x in range(len(cores)) if x != me and topo.same_plane(c, cores[x])]
    far = [x for x in range(len(cores)) if x != me and x not in near]
    part = [x for x in far if topo.may_write(c, cores[x]) and topo.chip(cores[x]) == topo.chip(c)][0]
    cross = [x for x in far if topo.may_write(c, cores[x]) and x != part][0]
    diag = [x for x in far if not topo.may_write(c, cores[x])]
    return near, part, cross, diag


def helpers(c, topo):
    return [h for h in range(512) if topo.host(h) == topo.host(c) and topo.chip(h) == topo.chip(c)
            and topo.die(h) != topo.die(c)][:2]


def places(cores, me, topo):
    near, part, cross, diag = roles(cores, me, topo)
    order = [part, cross] + near + [me] + diag
    return [order.index(o) for o in range(len(cores))]


def nbits(m):
    return bin(m).count("1")


def rank_program(g, core, T, topo):
    cores = [int(c) for c in T.cores]
    lsum = [0]

    def send(dsts, outs, src, sem):
        m = 0xFFFF
        ids = []
        for d in dsts:
            m &= topo.mask(core, d)
            rid, pid = topo.addr(d, core)
            ids.append(DstId(rid=rid, pnc=pid))
        g.remote_dma_fused([RemoteDMATransfer(dst_ids=ids, dma_engine_mask=m, remote_sem=T.sem[sem], srcs=[src],
                                              dsts=outs)], local_sem=T.sem.ls)
        lsum[0] += nbits(m)

    def block(o, t):
        at = 256 * places(cores, o, topo)[t]
        return T.ld[:, at:at + 256]

    me = T.rank_of(core)
    if me is None:
        own = [r for r in range(8) if topo.host(cores[r]) == topo.host(core) and topo.chip(cores[r]) == topo.chip(core)]
        if own and core in helpers(cores[own[0]], topo):
            p = roles(cores, own[0], topo)[1]
            to = roles(cores, p, topo)[3][helpers(cores[own[0]], topo).index(core)]
            g.wait_ge(T.sem.hx, nbits(topo.mask(cores[p], core)))
            send([cores[to]], [block(to, p)], T.fb[:, 0:256], "dn%d" % p)
            g.wait_ge(T.sem.ls, lsum[0])
        return
    near, part, cross, diag = roles(cores, me, topo)
    passed = roles(cores, part, topo)[3]
    pos = places(cores, me, topo)
    V, S, PE, SY = g.vector, g.scalar, g.tensor, g.sync
    nev = [0]
    waited = {}

    def ev():
        nev[0] += 1
        return ["e%d" % (nev[0] - 1), 0]

    def inc(ins, e, n=1):
        ins.then_inc(T.sem[e[0]], n)
        e[1] += n
        return e

    def one(ins, n=1):
        return inc(ins, ev(), n)

    def need(q, *es):
        nm = [k for k, v in (("g", g), ("v", V), ("s", S), ("p", PE), ("y", SY)) if v is q][0]
        for e in es:
            if waited.get((nm, e[0]), 0) < e[1]:
                q.wait_ge(T.sem[e[0]], e[1])
                waited[(nm, e[0])] = e[1]

    def arr(sem, o):
        src = o if topo.may_write(cores[o], core) else roles(cores, o, topo)[1]
        return [sem, nbits(topo.mask(cores[src], core))]

    def f(k):
        return T.fw[:, 64 * k:64 * k + 64]

    def w(k):
        return T.iw[:, 64 * k:64 * k + 64]

    s1, s2, rsum, rsb, off, nf, k8, zz = [f(k) for k in range(8)]
    vi, hh, si, lane, key = [w(k) for k in range(5)]
    t0, t1, t2, t3 = [T.tw[:, 16 * k:16 * k + 16] for k in range(4)]

    e_idx = ev()
    inc(SY.dma_start(T.pidx[0:64, :], T.idx[:, :]), e_idx, 16)
    inc(S.dma_start(T.pidx[64:128, :], T.idx[:, :]), e_idx, 16)
    e_map = ev()
    for k in range(4):
        inc(SY.dma_start(T.mapw[16 * k:16 * k + 16, :], T.mp[0:8, :]), e_map, 16)
        inc(S.dma_start(T.mapw[64 + 16 * k:80 + 16 * k, :], T.mp[8:16, :]), e_map, 16)

    e_pc = one(g.iota(T.pc[:, :], [[1, 1]], 0, 1))
    e_ic = one(g.iota(T.ic[:, :], [[1, 256]], 0, 0))
    ci, cf = T.ci, T.cf
    need(V, e_pc)
    x = ev()
    inc(V.tensor_scalar(ci[:, 0:1], T.pc[:, :], 1, None, OP.bitwise_and), x)
    inc(V.tensor_scalar(ci[:, 1:2], T.pc[:, :], 1, 7, OP.logical_shift_right, OP.bitwise_and), x)
    inc(V.tensor_scalar(ci[:, 2:3], T.pc[:, :], 3, 8, OP.logical_shift_right, OP.bitwise_and), x)
    inc(V.tensor_scalar(ci[:, 3:4], T.pc[:, :], 4, 3, OP.logical_shift_right, OP.bitwise_and), x)
    need(V, x)
    x = ev()
    inc(V.tensor_scalar(cf[:, 0:1], ci[:, 0:1], 16, 32 * me, OP.mult, OP.add), x)
    inc(V.tensor_tensor(cf[:, 1:2], ci[:, 1:2], ci[:, 2:3], OP.add), x)
    inc(V.tensor_copy(cf[:, 3:4], ci[:, 3:4]), x)
    need(V, x)
    x = one(V.tensor_tensor(cf[:, 2:3], cf[:, 0:1], cf[:, 1:2], OP.add))
    need(V, x, e_ic)
    e_w2 = one(V.tensor_scalar(T.w2[:, :], T.ic[:, :], cf[:, 2:3], None, OP.is_equal))
    e_ks = one(V.tensor_scalar(T.ks[:, :], T.ic[:, 0:4], cf[:, 3:4], None, OP.is_equal))

    need(V, e_idx)
    xb, xa = ev(), ev()
    inc(V.tensor_scalar(t1, T.pidx[:, :], 12, 240, OP.logical_shift_right, OP.bitwise_and), xb)
    inc(V.tensor_scalar(t2, T.pidx[:, :], 15, None, OP.bitwise_and), xb)
    inc(V.tensor_scalar(t0, T.pidx[:, :], 4, 4095, OP.logical_shift_right, OP.bitwise_and), xa)
    need(V, xb)
    xc = one(V.tensor_tensor(t3, t1, t2, OP.add))
    need(V, xa)
    e_msg = ev()
    lo = 32 * me
    inc(V.tensor_copy(T.lm[:, lo:lo + 16], t0), e_msg)
    need(V, xc)
    inc(V.tensor_copy(T.lm[:, lo + 16:lo + 32], t3), e_msg)

    need(g, e_msg)
    own_msg = T.lm[:, lo:lo + 32]
    send([cores[o] for o in [part, cross] + near], [own_msg] * 5, own_msg, "ix%d" % me)
    e_ix = {o: arr("ix%d" % o, o) for o in range(8) if o != me}
    need(g, e_ix[part])
    pm = T.lm[:, 32 * part:32 * part + 32]
    send([cores[o] for o in passed], [pm] * 2, pm, "ix%d" % part)
    gate0 = ev()
    g.sem_inc(T.sem[gate0[0]], 1)
    gate0[1] = 1
    e_tab = ev()
    need(SY, gate0)
    inc(SY.dma_start(T.tabw[:, 0:4096], T.tab[:, 0:4096]), e_tab, 16)

    x = ev()
    e_pf = one(V.tensor_copy(cf[:, 4:5], T.pc[:, :]))
    inc(V.tensor_scalar(ci[:, 5:6], T.pc[:, :], 2, 3, OP.logical_shift_right, OP.bitwise_and), x)
    inc(V.tensor_scalar(ci[:, 6:7], T.pc[:, :], 3, None, OP.bitwise_and), x)
    inc(V.tensor_scalar(ci[:, 7:8], T.pc[:, :], 4, None, OP.logical_shift_right), x)
    inc(V.tensor_scalar(T.r7[:, :], T.ic[:, 0:64], 7, None, OP.bitwise_and), x)
    inc(V.tensor_scalar(T.m15[:, :], T.ic[:, 0:128], 15, None, OP.bitwise_and), x)
    need(V, e_pf, x)
    e_c1, x = ev(), ev()
    inc(V.tensor_scalar(T.m1[:, :], T.ic[:, 0:128], cf[:, 4:5], -1.0, OP.is_le, OP.mult), e_c1)
    inc(V.memset(T.ones[:, :], 1.0), e_c1)
    inc(V.tensor_scalar(T.rst[:, :], T.r7[:, :], 0, None, OP.is_gt), e_c1)
    inc(V.tensor_scalar(T.rep[0:16, :], T.m15[0:16, :], cf[0:16, 4:5], None, OP.is_equal), e_c1)
    inc(V.tensor_copy(cf[:, 5:6], ci[:, 5:6]), x)
    inc(V.tensor_scalar(cf[:, 6:7], ci[:, 6:7], 16, None, OP.mult), x)
    need(V, x)
    x = one(V.tensor_tensor(cf[:, 7:8], cf[:, 6:7], ci[:, 7:8], OP.add))
    e_c2 = ev()
    for k in range(4):
        inc(V.tensor_scalar(T.lk[:, 128 * k:128 * k + 128], T.m15[:, :], cf[:, 5:6], 4 * k, OP.subtract, OP.is_equal), e_c2)
    need(V, x)
    for d in range(2):
        inc(V.tensor_scalar(T.cd[:, 64 * d:64 * d + 64], T.ic[:, 0:64], cf[:, 7:8], 8 * d, OP.subtract, OP.is_equal), e_c2)
    for o in range(8):
        inc(V.memset(T.posr[:, 8 * o:8 * o + 8], 2.0 * pos[o]), e_c2)

    need(S, e_w2)
    need(PE, e_ks)
    need(V, e_map)
    e_pv = ev()
    for i in [me] + near + [part, cross] + diag:
        src = e_msg if i == me else e_ix[i]
        b, mb = 32 * i, 256 * i
        need(S, src)
        xm = one(S.activation(T.mk[:, mb:mb + 256], T.w2[:, :].indirect(T.lm[:, b + 16:b + 32]), COPY))
        need(V, src, xm)
        xp = one(V.tensor_tensor(T.pr[:, mb:mb + 256], T.mapw[:, :].indirect(T.lm[:, b:b + 16]), T.mk[:, mb:mb + 256], OP.mult))
        need(PE, xp)
        for d in range(2):
            c0 = 8 * i + 4 * d
            inc(PE.matmul(T.pv[:, c0:c0 + 4], T.pr[:, mb + 128 * d:mb + 128 * d + 128], T.ks[:, :], True, True), e_pv)

    need(V, e_pv)
    e_vs = one(V.tensor_copy(T.vs[:, :], T.pv[:, 0:64]))
    need(g, e_vs)
    vl = T.vl[:, 64 * me:64 * me + 64]
    send([cores[o] for o in near], [vl] * 3, T.vs[:, :], "vn%d" % me)
    gate1 = ev()
    g.sem_inc(T.sem[gate1[0]], 1)
    gate1[1] = 1
    need(SY, gate1)
    inc(SY.dma_start(T.tabw[:, 4096:8192], T.tab[:, 4096:8192]), e_tab, 16)
    na, nb, nc = near
    need(V, e_vs)
    for o in near:
        need(V, arr("vn%d" % o, o))
    x = ev()
    inc(V.tensor_tensor(s1, T.vl[:, 64 * na:64 * na + 64], T.vl[:, 64 * nb:64 * nb + 64], OP.add), x)
    inc(V.tensor_tensor(s2, T.vs[:, :], T.vl[:, 64 * nc:64 * nc + 64], OP.add), x)
    need(V, x)
    e_rs = one(V.tensor_tensor(rsum, s1, s2, OP.add))
    need(g, e_rs)
    send([cores[part]], [T.vq[:, :]], rsum, "vp")
    need(V, e_rs)
    e_rb = one(V.tensor_scalar(rsb, rsum, -1, 8192 * me, OP.mult, OP.add))
    need(V, arr("vp", part))
    x = one(V.tensor_tensor(vi, rsum, T.vq[:, :], OP.add))
    need(V, e_rb)
    e_off = one(V.tensor_tensor(off, rsb, T.vq[:, :], OP.subtract))

    need(V, x)
    e_h = one(V.tensor_scalar(hh, vi, 13, None, OP.logical_shift_right))
    need(V, e_h, e_c1)
    e_f = one(V.tensor_scalar(T.ff[:, :], hh, me, None, OP.is_equal))
    e_nf = one(V.tensor_scalar(nf, hh, me, 4096, OP.not_equal, OP.mult))
    need(V, e_f)
    e_fi = one(V.tensor_tensor_scan(T.fi[:, :], T.rst[:, :], T.ff[:, :], 0.0, OP.mult, OP.add))
    need(PE, e_c1, e_f)
    PE.matmul(T.prk[:, 0:64], T.m1[:, :], T.ff[:, :], True, False)
    need(PE, e_fi)
    e_rk = one(PE.matmul(T.prk[:, 0:64], T.ones[:, :], T.fi[:, :], False, True))
    need(V, e_rk, e_nf)
    x = one(V.tensor_tensor(si, T.prk[:, 0:64], nf, OP.add))
    need(V, x)
    xk = one(V.tensor_scalar(key, si, 4, None, OP.logical_shift_right))
    xl = one(V.tensor_scalar(lane, si, 4096 + 15, None, OP.bitwise_and))
    e_ab = [ev(), ev()]

    def lanes(m0, m1):
        for m in range(m0, m1):
            inc(V.tensor_scalar(T.aa[:, 64 * m:64 * m + 64], lane, m, None, OP.is_equal), e_ab[0])

    need(V, xk)
    x8 = one(V.tensor_scalar(k8, key, -8192, None, OP.mult))
    need(V, xl)
    lanes(0, 1)
    need(V, x8, e_off)
    xz = one(V.tensor_tensor(zz, k8, off, OP.add))
    lanes(1, 16)
    need(V, xz)
    for n in range(8):
        inc(V.tensor_scalar(T.bb[:, 64 * n:64 * n + 64], zz, -8192 * n - 8192, -8192 * n, OP.max, OP.min), e_ab[0])
    need(S, xz)
    xs = ev()
    for n in range(8, 16):
        inc(S.activation(T.bt[:, 64 * n - 512:64 * n - 448], zz, RELU, bias=-8192.0 * n, scale=-1.0), xs)
    need(S, xs)
    for n in range(8, 16):
        inc(S.activation(T.bb[:, 64 * n:64 * n + 64], T.bt[:, 64 * n - 512:64 * n - 448], RELU, bias=8192.0, scale=-1.0), e_ab[1])
    batches = [diag, [cross, part], near[0:2], [near[2], me]]
    px, po = [T.px0, T.px1, T.pv, T.px0], [T.po0, T.po1, T.po0, T.po1]
    e_x, e_o, e_xf, e_ou = [ev() for b in range(4)], [None] * 4, [None] * 4, [None] * 4

    def pack(b, j, n0=0, n1=16):
        for c in range(8):
            col = 8 * batches[b][j] + c
            ins = PE.matmul(px[b][0:16, 16 * j + n0:16 * j + n1], T.aa[:, col:1024:64],
                            T.bb[:, 64 * n0 + col:64 * n1:64], c == 0, c == 7)
        inc(ins, e_x[b])

    def strip(b):
        s = slice(32 * b, 32 * b + 32)
        need(V, e_x[b])
        x = one(V.tensor_scalar(T.xi[0:16, s], px[b][0:16, 0:32], -1, None, OP.mult))
        need(V, x)
        x = one(V.tensor_scalar(T.xm[0:16, s], T.xi[0:16, s], 8191, None, OP.bitwise_and))
        need(V, x)
        e_xf[b] = one(V.tensor_copy(T.xf[0:16, s], T.xm[0:16, s]))

    def spread(b):
        need(PE, e_xf[b])
        if b >= 2:
            need(PE, e_ou[b - 2])
        e_o[b] = one(PE.matmul(po[b][:, 0:32], T.rep[0:16, :], T.xf[0:16, 32 * b:32 * b + 32], True, True))

    e_c = {}

    def columns(b):
        need(V, e_o[b])
        e_ou[b] = one(V.tensor_copy(T.ou[:, 32 * b:32 * b + 32], po[b][:, 0:32]))
        need(V, e_ou[b], e_tab)
        need(S, e_ou[b], e_tab)
        for j, i in enumerate(batches[b]):
            src = T.tabw[:, :].indirect(T.ou[:, 32 * b + 16 * j:32 * b + 16 * j + 16])
            dst = block(me, me) if i == me else T.fb[:, 512 * b + 256 * j:512 * b + 256 * j + 256]
            e_c[i] = one(S.activation(dst, src, COPY) if j else V.tensor_copy(dst, src))

    need(PE, e_ab[0])
    pack(0, 0, 0, 8)
    pack(0, 1, 0, 8)
    need(PE, e_ab[1])
    pack(0, 0, 8, 16)
    pack(0, 1, 8, 16)
    e_fr = ev()
    hm = T.iw[:, 64 + 8 * me:72 + 8 * me]
    for o in range(8):
        inc(V.tensor_scalar(T.fr[:, 8 * o:8 * o + 8], hm, o, None, OP.is_equal), e_fr)
    strip(0)
    pack(1, 0)
    spread(0)
    columns(0)
    pack(1, 1)
    strip(1)
    need(V, e_fr)
    e_fri = one(V.tensor_tensor_scan(T.fri[:, :], T.rst[:, :], T.fr[:, :], 0.0, OP.mult, OP.add))
    pack(2, 0)
    spread(1)
    columns(1)
    pack(2, 1)
    need(PE, e_fr, e_c2, e_fri)
    PE.matmul(T.prk2[:, 0:64], T.m1[:, :], T.fr[:, :], True, False)
    PE.matmul(T.prk2[:, 0:64], T.ones[:, :], T.posr[:, :], False, False)
    e_p2 = one(PE.matmul(T.prk2[:, 0:64], T.ones[:, :], T.fri[:, :], False, True))
    strip(2)
    pack(3, 0)
    spread(2)
    columns(2)
    pack(3, 1)
    strip(3)
    spread(3)
    columns(3)

    for k, i in enumerate(diag + [cross, part] + near):
        need(g, e_c[i])
        src = T.fb[:, 256 * k:256 * k + 256]
        if i in diag:
            send([helpers(cores[part], topo)[k]], [T.fb[:, 0:256]], src, "hx")
        else:
            send([cores[i]], [block(i, me)], src, "dn%d" % me)

    need(V, e_p2, e_fr)
    x = one(V.tensor_tensor(T.r2[:, :], T.prk2[:, 0:64], T.fr[:, :], OP.mult))
    need(V, x)
    x = one(V.tensor_tensor(T.uw[:, 0:32], T.r2[:, 0:32], T.r2[:, 32:64], OP.add))
    need(V, x)
    x = one(V.tensor_tensor(T.uw[:, 32:48], T.uw[:, 0:16], T.uw[:, 16:32], OP.add))
    need(V, x)
    x = one(V.tensor_tensor(T.uw[:, 48:56], T.uw[:, 32:40], T.uw[:, 40:48], OP.add))
    need(S, x, e_c2)
    for d in range(2):
        for k in range(4):
            j = 4 * d + k
            xs = one(S.activation(T.cs[:, 64 * j:64 * j + 64], T.cd[:, 64 * d:64 * d + 64], COPY, scale=T.uw[:, 48 + j:49 + j]))
            need(PE, xs)
            ins = PE.matmul(T.ppo[:, 0:64], T.lk[:, 128 * k:128 * k + 128], T.cs[:, 64 * j:64 * j + 64], j == 0, j == 7)
    e_po = one(ins)
    need(V, e_po)
    e_pou = one(V.tensor_copy(T.pou[:, :], T.ppo[:, 0:64]))
    win = T.ld[:, 0:2048]
    for q in (V, S):
        need(q, e_pou, e_c[me])
        for o in near + [cross, part] + diag:
            need(q, arr("dn%d" % o, o))
    ya = one(V.tensor_copy(T.yy[:, 0:512], win.indirect(T.pou[:, 0:32])))
    yb = one(S.activation(T.yy[:, 512:1024], win.indirect(T.pou[:, 32:64]), COPY))
    need(SY, ya)
    need(S, yb)
    e_y = ev()
    inc(SY.dma_start(T.y[:, 0:512], T.yy[:, 0:512]), e_y, 16)
    inc(S.dma_start(T.y[:, 512:1024], T.yy[:, 512:1024]), e_y, 16)
    g.wait_ge(T.sem.ls, lsum[0])
    need(g, e_y)
